import numpy as np
import ml_dtypes


def mxq(x, axis, fmt="e4m3"):
    dtype, down = {"e4m3": (ml_dtypes.float8_e4m3fn, 7), "e5m2": (ml_dtypes.float8_e5m2, 14)}[fmt]
    v = np.moveaxis(np.asarray(x, np.float32).astype(ml_dtypes.bfloat16).astype(np.float64), axis, -1)
    blocks = v.reshape(v.shape[:-1] + (-1, 32))
    amax = np.abs(blocks).max(-1, keepdims=True)
    byte = np.maximum(np.where(amax > 0, np.frexp(amax)[1] - 1 + 127, 0) - down, 1)
    scale = np.exp2(byte - 127.0)
    codes = (blocks / scale).astype(np.float32).astype(dtype).astype(np.float64)
    return np.moveaxis((codes * scale).reshape(v.shape), -1, axis)


WIDE = False


def mx_kscale(k):
    if not WIDE:
        return np.ones(k)
    levels = np.array([24, -24, 12, -12, 0])
    if k % 512:
        return np.exp2(np.random.permutation(np.resize(levels, k // 32))).repeat(32)
    a = np.empty((k // 512, 16))
    for p in range(k // 512):
        a[p, :8] = np.random.permutation(np.resize(levels, 8))
        for g in range(8):
            far = levels[np.abs(levels - a[p, g]) >= 10]
            a[p, g + 8] = far[np.random.randint(len(far))]
    return np.exp2(a.ravel()).repeat(32)


def f64(x):
    return np.asarray(x).astype(np.float64)


def striped8(idx):
    return np.concatenate([v.reshape(-1, 16).T for v in idx]).astype(np.uint16)


def unstriped8(offs):
    return np.stack([offs[16 * g:16 * g + 16].T.reshape(-1) for g in range(8)]).astype(np.int64)


E2M1 = np.array([0.0, 0.5, 1.0, 1.5, 2.0, 3.0, 4.0, 6.0, -0.0, -0.5, -1.0, -1.5, -2.0, -3.0, -4.0, -6.0])


def pack_weight(w, fmt):
    k, n = w.shape
    w = f64(np.asarray(w, np.float32).astype(ml_dtypes.bfloat16)).reshape(k // 32, 32, n)
    amax = np.abs(w).max(1)
    if fmt == "e4m3":
        byte = np.frexp(amax)[1] - 1 + 127 - 7
    else:
        mant, ex = np.frexp(amax / 6.0)
        byte = np.where(mant > 0.5, ex, ex - 1) + 127
    byte = np.clip(np.where(amax > 0, byte, 1), 1, 254)
    scaled = (w * np.exp2(127.0 - byte)[:, None, :]).reshape(k, n).astype(np.float32)
    by_word = np.ascontiguousarray(scaled.reshape(k // 512, 128, 4, n).transpose(0, 1, 3, 2))
    if fmt == "e4m3":
        words = by_word.astype(ml_dtypes.float8_e4m3fn).view(np.uint8)
    else:
        c = by_word.astype(ml_dtypes.float4_e2m1fn).view(np.uint8) & 0xF
        words = (c[..., 0::2] | (c[..., 1::2] << 4)).reshape(k // 512, 128, 2 * n)
    return np.ascontiguousarray(words), np.ascontiguousarray(byte.astype(np.uint8).reshape(k // 512, 16, n))


def unpack_weight(words, scales, fmt):
    g, _, n = scales.shape
    words = np.ascontiguousarray(words).reshape(g, 128, n, -1)
    if fmt == "e4m3":
        vals = words.view(ml_dtypes.float8_e4m3fn).astype(np.float64)
    else:
        nib = np.empty((g, 128, n, 4), np.uint8)
        nib[..., 0::2] = words & 0xF
        nib[..., 1::2] = words >> 4
        vals = E2M1[nib]
    vals = vals * np.repeat(np.exp2(scales.astype(np.float64) - 127.0), 8, axis=1)[..., None]
    return vals.transpose(0, 1, 3, 2).reshape(g * 512, n)


K, L, N, T, J = 1024, 512, 512, 2048, 1024


def setup_inputs():
    n = np.random.standard_normal
    s = mx_kscale(K)[:, None]
    s2 = mx_kscale(L)[:, None]
    p_wx = pack_weight(n((L, N)) / np.sqrt(L) / s2, "e2m1")
    return {
        "xT": (n((K, T)) * s).astype(np.float32),
        "wgt": np.repeat(np.random.uniform(0.5, 2.0, (8, J)), 16, axis=0).astype(np.float32),
        "wt": (n((K, N)) / np.sqrt(K) / s).astype(np.float32),
        "c": (n((L, J)) * s2).astype(np.float32),
        "wx_words": p_wx[0],
        "wx_scales": p_wx[1],
        "offs": striped8(np.stack([np.random.permutation(T)[:J] for _ in range(8)])),
    }


def reference(xT, wgt, wt, c, wx_words, wx_scales, offs):
    idx = unstriped8(offs)
    rows = np.arange(K)
    xg = f64(wgt)[rows // 4 % 128] * f64(xT)[rows[:, None], idx[rows % 512 // 64]]
    xT_ = mxq(xg, 0, "e4m3")
    wt_ = mxq(f64(wt), 0, "e4m3")
    c_q_ = mxq(f64(c), 0, "e4m3")
    c_r_ = mxq(f64(c) - c_q_, 0, "e4m3")
    wx_ = unpack_weight(wx_words, wx_scales, "e2m1")
    y = wt_.T @ xT_ + wx_.T @ c_q_ + wx_.T @ c_r_
    return y

@@ -1,0 +1,249 @@
+import concourse.mybir as mybir
+from concourse.masks import make_identity
+
+K, L, N, T, J = 1024, 512, 512, 2048, 1024
+FLOPS = 2 * (K * N * J + 2 * L * N * J + L * L * J)
+
+F32 = mybir.dt.float32
+BF16 = mybir.dt.bfloat16
+I32 = mybir.dt.int32
+U32 = mybir.dt.uint32
+U16 = mybir.dt.uint16
+U8 = mybir.dt.uint8
+FP8X4 = mybir.dt.float8_e4m3fn_x4
+FP4X4 = mybir.dt.float4_e2m1fn_x4
+MULT = mybir.AluOpType.mult
+SUB = mybir.AluOpType.subtract
+
+P = 128
+HALF = 512
+QUART = 256
+
+
+def tile_list_none_kernel(tc, xT, wgt, wt, c, wx_words, wx_scales, offs, out):
+    nc = tc.nc
+    with tc.tile_pool(name="keep", bufs=1) as keep, tc.psum_pool(name="psum", bufs=1) as psum:
+        offsets = keep.tile([P, J // 16], U16, name="offsets")
+        nc.sync.dma_start(offsets[:], offs)
+
+        def mx_tiles(name, width):
+            rounded = keep.tile([P, width, 4], BF16, name=name + "_bf", align_bytes=64)
+            codes = keep.tile([P, width], U32, name=name + "_codes", align_bytes=64)
+            scales = keep.tile([P, width], U8, name=name + "_scales", align_bytes=64)
+            return rounded, codes, scales
+
+        def quantize(op, a, b):
+            rounded, codes, scales = op
+            nc.vector.quantize_mx(
+                out=codes[:, a:b].bitcast(FP8X4),
+                scales=scales[:, a:b],
+                in_=rounded[:, a:b, :].rearrange("p w t -> p (w t)"),
+            )
+
+        def by_fours(ap_wt):
+            return ap_wt.rearrange("p (c i) t -> p c t i", i=4)
+
+        def planes_by_fours(ap_tw):
+            return ap_tw.rearrange("p t (c i) -> p c t i", i=4)
+
+        x_planes = [keep.tile([P, T], F32, name="x%d" % g) for g in range(8)]
+        picked = [keep.tile([P, 4, J], F32, name="picked%d" % a) for a in range(2)]
+        wgt_sb = keep.tile([P, J], F32, name="wgt_sb")
+        wt_raw = [keep.tile([P, 4, N], F32, name="wt_raw%d" % a) for a in range(2)]
+        c_raw = [keep.tile([P, 4, QUART], F32, name="c_raw%d" % q) for q in range(4)]
+        wx_codes = keep.tile([P, 2 * N], U8, name="wx_codes", align_bytes=256)
+        wx_plane = keep.tile([P, N], U8, name="wx_plane", align_bytes=64)
+        xg = [mx_tiles("xg%d" % a, J) for a in range(2)]
+        wq = [mx_tiles("wq%d" % a, N) for a in range(2)]
+        cq = mx_tiles("cq", J)
+        cr = mx_tiles("cr", J)
+        staged = [keep.tile([P, HALF], F32, name="staged%d" % b) for b in range(8)]
+
+        eye = keep.tile([P, P], BF16, name="eye")
+        make_identity(nc, eye[:])
+        eye_bf = keep.tile([P, 4 * HALF], BF16, name="eye_bf", align_bytes=64)
+        eye_codes = keep.tile([P, HALF], U32, name="eye_codes", align_bytes=64)
+        eye_scales = keep.tile([P, HALF], U8, name="eye_scales", align_bytes=64)
+        nc.vector.memset(eye_bf[:].bitcast(I32), 0)
+        nc.vector.memset(wx_plane[:].bitcast(I32), 0)
+        for t in range(4):
+            diag = eye_bf[:, HALF * t + t : HALF * (t + 1) : 4]
+            if t == 0:
+                nc.scalar.copy(diag, eye[:])
+            else:
+                nc.vector.tensor_copy(diag, eye[:])
+        nc.vector.quantize_mx(out=eye_codes[:].bitcast(FP8X4), scales=eye_scales[:], in_=eye_bf[:])
+
+        c_view = c.rearrange("(p t) j -> p t j", t=4)
+
+        def load_x(g):
+            a, t = divmod(g, 4)
+            rows = xT[HALF * a : HALF * (a + 1), :].rearrange("(p t) w -> p t w", t=4)
+            nc.sync.dma_start(x_planes[g][:], rows[:, t, :])
+
+        def load_c(q):
+            nc.sync.dma_start(c_raw[q][:], c_view[:, :, QUART * q : QUART * (q + 1)])
+
+        def load_wgt(h):
+            nc.sync.dma_start(wgt_sb[:, HALF * h : HALF * (h + 1)], wgt[:, HALF * h : HALF * (h + 1)])
+
+        def load_wt(a):
+            nc.sync.dma_start(wt_raw[a][:], wt[HALF * a : HALF * (a + 1), :].rearrange("(p t) n -> p t n", t=4))
+
+        def load_wx():
+            nc.sync.dma_start(wx_codes[:].bitcast(I32), wx_words[0].bitcast(I32))
+            for quad in range(4):
+                nc.sync.dma_start(
+                    wx_plane[32 * quad : 32 * quad + 4, :].bitcast(I32),
+                    wx_scales[0, 4 * quad : 4 * quad + 4, :].bitcast(I32),
+                )
+
+        load_c(0)
+        load_wgt(0)
+        load_x(0)
+        load_wgt(1)
+        load_x(1)
+        load_c(1)
+        load_x(2)
+        load_c(2)
+        load_x(3)
+        load_c(3)
+        load_wx()
+        load_wt(0)
+        load_x(4)
+        load_x(5)
+        load_x(6)
+        load_wt(1)
+        load_x(7)
+
+        def gather(g, a, b):
+            nc.vector.tensor_tensor(
+                picked[g // 4][:, g % 4, a:b],
+                x_planes[g][:].indirect(offsets[:, a // 16 : b // 16]),
+                wgt_sb[:, a:b],
+                MULT,
+            )
+
+        def round_c(q):
+            nc.scalar.copy(by_fours(cq[0][:, QUART * q : QUART * (q + 1), :]), planes_by_fours(c_raw[q][:]))
+
+        decoded = {}
+
+        def decode(e):
+            bank = psum.tile([P, HALF], F32, name="dec%d" % e, tag="bank%d" % (4 + e % 4))
+            decoded[e] = bank
+            for t in range(4):
+                nc.tensor.matmul_mx(
+                    out=bank[:, P * t : P * (t + 1)],
+                    lhsT=eye_codes[:, P * t : P * (t + 1)].bitcast(FP8X4),
+                    lhsT_scale=eye_scales[:, P * t : P * (t + 1)],
+                    rhs=cq[1][:, P * e : P * (e + 1)].bitcast(FP8X4),
+                    rhs_scale=cq[2][:, P * e : P * (e + 1)],
+                    start=True,
+                    stop=True,
+                )
+
+        def leftover(e):
+            q, o = divmod(e, 2)
+            nc.vector.tensor_tensor(
+                by_fours(cr[0][:, P * e : P * (e + 1), :]),
+                planes_by_fours(c_raw[q][:, :, P * o : P * (o + 1)]),
+                decoded[e][:].rearrange("p (t c i) -> p c t i", t=4, i=4),
+                SUB,
+            )
+
+        def quant_cq(q):
+            quantize(cq, QUART * q, QUART * (q + 1))
+            decode(2 * q)
+            decode(2 * q + 1)
+
+        def finish_c(q):
+            leftover(2 * q)
+            leftover(2 * q + 1)
+
+        def round_all(dst, src, a, b):
+            nc.scalar.copy(by_fours(dst[:, a:b, :]), planes_by_fours(src[:, :, a:b]))
+
+        def round_pair(copy, u, a, b):
+            copy(xg[1][0][:, a:b, 2 * u : 2 * u + 2], picked[1][:, 2 * u : 2 * u + 2, a:b].rearrange("p t w -> p w t"))
+
+        acc = {}
+
+        def wx_pass(h, n, op, start):
+            if start:
+                acc[h, n] = psum.tile([P, HALF], F32, name="acc%d%d" % (h, n), tag="bank%d" % (4 * h + n))
+            nc.tensor.matmul_mx(
+                out=acc[h, n][:],
+                lhsT=wx_codes[:, 2 * P * n : 2 * P * (n + 1)].bitcast(FP4X4),
+                lhsT_scale=wx_plane[:, P * n : P * (n + 1)],
+                rhs=op[1][:, HALF * h : HALF * (h + 1)].bitcast(FP8X4),
+                rhs_scale=op[2][:, HALF * h : HALF * (h + 1)],
+                start=start,
+                stop=False,
+            )
+
+        def wt_pass(a, n, lo, hi, stop):
+            h = lo // HALF
+            nc.tensor.matmul_mx(
+                out=acc[h, n][:, lo - HALF * h : hi - HALF * h],
+                lhsT=wq[a][1][:, P * n : P * (n + 1)].bitcast(FP8X4),
+                lhsT_scale=wq[a][2][:, P * n : P * (n + 1)],
+                rhs=xg[a][1][:, lo:hi].bitcast(FP8X4),
+                rhs_scale=xg[a][2][:, lo:hi],
+                start=False,
+                stop=stop,
+            )
+
+        def emit(h, n, copy):
+            copy(staged[4 * h + n][:], acc[h, n][:])
+            nc.sync.dma_start(out[P * n : P * (n + 1), HALF * h : HALF * (h + 1)], staged[4 * h + n][:])
+
+        for q in range(4):
+            round_c(q)
+            quant_cq(q)
+            if q > 0:
+                gather(q - 1, HALF, J)
+            finish_c(q)
+            gather(q, 0, HALF)
+            quantize(cr, QUART * q, QUART * (q + 1))
+        gather(3, HALF, J)
+        for h in range(2):
+            round_all(xg[0][0], picked[0], HALF * h, HALF * (h + 1))
+        round_all(wq[0][0], wt_raw[0], 0, N)
+        for h in range(2):
+            for n in range(4):
+                wx_pass(h, n, cq, True)
+                wx_pass(h, n, cr, False)
+        gather(4, 0, HALF)
+        gather(4, HALF, J)
+        quantize(xg[0], 0, HALF)
+        gather(5, 0, HALF)
+        quantize(xg[0], HALF, J)
+        gather(5, HALF, J)
+        quantize(wq[0], 0, N)
+        for h in range(2):
+            for n in range(4):
+                wt_pass(0, n, HALF * h, HALF * (h + 1), False)
+        round_pair(nc.scalar.copy, 0, 0, J)
+        gather(6, 0, HALF)
+        gather(6, HALF, J)
+        round_all(wq[1][0], wt_raw[1], 0, N)
+        quantize(wq[1], 0, N)
+        for q in range(4):
+            gather(7, QUART * q, QUART * (q + 1))
+        round_pair(nc.scalar.copy, 1, 0, QUART)
+        round_pair(nc.scalar.copy, 1, QUART, HALF)
+        quantize(xg[1], 0, QUART)
+        quantize(xg[1], QUART, HALF)
+        round_pair(nc.vector.tensor_copy, 1, HALF, J)
+        for n in range(4):
+            wt_pass(1, n, 0, QUART, False)
+        for n in range(4):
+            wt_pass(1, n, QUART, HALF, True)
+        quantize(xg[1], HALF, J)
+        for n in range(4):
+            wt_pass(1, n, HALF, J, True)
+        for n in range(4):
+            emit(0, n, nc.scalar.copy)
+        for n in range(4):
+            emit(1, n, nc.vector.tensor_copy if n % 2 == 0 else nc.scalar.copy)

@@ -12,238 +12,329 @@ U16 = mybir.dt.uint16
 U8 = mybir.dt.uint8
 FP8X4 = mybir.dt.float8_e4m3fn_x4
 FP4X4 = mybir.dt.float4_e2m1fn_x4
-MULT = mybir.AluOpType.mult
-SUB = mybir.AluOpType.subtract
+ALU = mybir.AluOpType
 
 P = 128
-HALF = 512
-QUART = 256
+PACK = 4
+PASS = P * PACK
+BANK = 512
+BANKS = 8
+ROW_TILES = N // P
+LIST_ROWS = 16
+RUN = 4
+HALF = J // 2
+QUARTER = J // 4
+
+FRONT, MIDDLE, LAST = (0, HALF), (HALF, HALF + QUARTER), (HALF + QUARTER, J)
+BACK = (HALF, J)
+FIRST_BANK = {FRONT: 0, MIDDLE: ROW_TILES, LAST: 0}
+ADDED_TILES, PLAIN_TILES = (2, 3), (0, 1)
+
+PICKED = [(0, 4, FRONT), (0, 4, BACK), (4, 6, FRONT), (6, 8, FRONT), (4, 8, MIDDLE), (4, 8, LAST)]
+
+TAKES_BYTES_OF = {
+    "cq_bf0": "eye_bf",
+    "cq_bf1": "eye",
+    "cq_bf2": "cq_bf0",
+    "cq_bf3": "cq_bf1",
+    "wt_bf0": "cq_bf3",
+    "wt_bf1": "x0",
+    "picked0_0": "c_raw512",
+    "picked0_512": "c_raw768",
+    "picked4_0": "x1",
+    "picked4_512": "x2",
+    "picked6_0": "xg_bf0_0",
+    "picked4_768": "picked6_0",
+}
 
 
 def tile_list_none_kernel(tc, xT, wgt, wt, c, wx_words, wx_scales, offs, out):
     nc = tc.nc
     with tc.tile_pool(name="keep", bufs=1) as keep, tc.psum_pool(name="psum", bufs=1) as psum:
-        offsets = keep.tile([P, J // 16], U16, name="offsets")
+        offsets = keep.tile([P, J // LIST_ROWS], U16, name="offsets")
         nc.sync.dma_start(offsets[:], offs)
 
-        def mx_tiles(name, width):
-            rounded = keep.tile([P, width, 4], BF16, name=name + "_bf", align_bytes=64)
+        buffers = {}
+
+        def buffer(name, shape, dtype):
+            if name not in buffers:
+                tag = name
+                while tag in TAKES_BYTES_OF:
+                    tag = TAKES_BYTES_OF[tag]
+                buffers[name] = keep.tile(shape, dtype, name=name, tag=tag, align_bytes=64)
+            return buffers[name]
+
+        def bank_tile(name, bank):
+            return psum.tile([P, BANK], F32, name=name, tag="bank%d" % bank)
+
+        def mx_operand(name, width):
             codes = keep.tile([P, width], U32, name=name + "_codes", align_bytes=64)
             scales = keep.tile([P, width], U8, name=name + "_scales", align_bytes=64)
-            return rounded, codes, scales
+            return codes, scales
 
-        def quantize(op, a, b):
-            rounded, codes, scales = op
+        def quantize(operand, cols, woven):
+            codes, scales = operand
             nc.vector.quantize_mx(
-                out=codes[:, a:b].bitcast(FP8X4),
-                scales=scales[:, a:b],
-                in_=rounded[:, a:b, :].rearrange("p w t -> p (w t)"),
+                out=codes[:, cols[0] : cols[1]].bitcast(FP8X4),
+                scales=scales[:, cols[0] : cols[1]],
+                in_=woven.rearrange("p w t -> p (w t)"),
             )
 
-        def by_fours(ap_wt):
-            return ap_wt.rearrange("p (c i) t -> p c t i", i=4)
+        def columns_in_runs(woven):
+            return woven.rearrange("p (c i) t -> p c t i", i=RUN)
 
-        def planes_by_fours(ap_tw):
-            return ap_tw.rearrange("p t (c i) -> p c t i", i=4)
+        def planes_in_runs(planes):
+            return planes.rearrange("p t (c i) -> p c t i", i=RUN)
 
-        x_planes = [keep.tile([P, T], F32, name="x%d" % g) for g in range(8)]
-        picked = [keep.tile([P, 4, J], F32, name="picked%d" % a) for a in range(2)]
+        def matmul(result, stationary, moving, cols, start, stop):
+            nc.tensor.matmul_mx(
+                out=result,
+                lhsT=stationary[0],
+                lhsT_scale=stationary[1],
+                rhs=moving[0][:, cols[0] : cols[1]].bitcast(FP8X4),
+                rhs_scale=moving[1][:, cols[0] : cols[1]],
+                start=start,
+                stop=stop,
+            )
+
+        def e4m3_columns(operand, n):
+            return operand[0][:, P * n : P * (n + 1)].bitcast(FP8X4), operand[1][:, P * n : P * (n + 1)]
+
         wgt_sb = keep.tile([P, J], F32, name="wgt_sb")
-        wt_raw = [keep.tile([P, 4, N], F32, name="wt_raw%d" % a) for a in range(2)]
-        c_raw = [keep.tile([P, 4, QUART], F32, name="c_raw%d" % q) for q in range(4)]
         wx_codes = keep.tile([P, 2 * N], U8, name="wx_codes", align_bytes=256)
-        wx_plane = keep.tile([P, N], U8, name="wx_plane", align_bytes=64)
-        xg = [mx_tiles("xg%d" % a, J) for a in range(2)]
-        wq = [mx_tiles("wq%d" % a, N) for a in range(2)]
-        cq = mx_tiles("cq", J)
-        cr = mx_tiles("cr", J)
-        staged = [keep.tile([P, HALF], F32, name="staged%d" % b) for b in range(8)]
+        wx_bytes = keep.tile([P, N], U8, name="wx_bytes", align_bytes=64)
+        xg = [mx_operand("xg%d" % a, J) for a in range(K // PASS)]
+        wq = [mx_operand("wq%d" % a, N) for a in range(K // PASS)]
+        cq = mx_operand("cq", J)
+        cr = mx_operand("cr", J)
 
-        eye = keep.tile([P, P], BF16, name="eye")
+        def wx_columns(n):
+            return wx_codes[:, 2 * P * n : 2 * P * (n + 1)].bitcast(FP4X4), wx_bytes[:, P * n : P * (n + 1)]
+
+        eye = buffer("eye", [P, P], BF16)
+        eye_bf = buffer("eye_bf", [P, PACK * PASS], BF16)
+        eye_mx = mx_operand("eye", PASS)
+        nc.gpsimd.memset(eye_bf[:, 0:PASS].bitcast(I32), 0)
         make_identity(nc, eye[:])
-        eye_bf = keep.tile([P, 4 * HALF], BF16, name="eye_bf", align_bytes=64)
-        eye_codes = keep.tile([P, HALF], U32, name="eye_codes", align_bytes=64)
-        eye_scales = keep.tile([P, HALF], U8, name="eye_scales", align_bytes=64)
-        nc.vector.memset(eye_bf[:].bitcast(I32), 0)
-        nc.vector.memset(wx_plane[:].bitcast(I32), 0)
-        for t in range(4):
-            diag = eye_bf[:, HALF * t + t : HALF * (t + 1) : 4]
-            if t == 0:
-                nc.scalar.copy(diag, eye[:])
-            else:
-                nc.vector.tensor_copy(diag, eye[:])
-        nc.vector.quantize_mx(out=eye_codes[:].bitcast(FP8X4), scales=eye_scales[:], in_=eye_bf[:])
+        nc.vector.memset(eye_bf[:, PASS:].bitcast(I32), 0)
+        nc.vector.memset(wx_bytes[:].bitcast(I32), 0)
+        for t in range(PACK):
+            copy = nc.scalar.copy if t == 0 else nc.vector.tensor_copy
+            copy(eye_bf[:, PASS * t + t : PASS * (t + 1) : PACK], eye[:])
+        nc.vector.quantize_mx(out=eye_mx[0][:].bitcast(FP8X4), scales=eye_mx[1][:], in_=eye_bf[:])
 
-        c_view = c.rearrange("(p t) j -> p t j", t=4)
-
-        def load_x(g):
-            a, t = divmod(g, 4)
-            rows = xT[HALF * a : HALF * (a + 1), :].rearrange("(p t) w -> p t w", t=4)
-            nc.sync.dma_start(x_planes[g][:], rows[:, t, :])
-
-        def load_c(q):
-            nc.sync.dma_start(c_raw[q][:], c_view[:, :, QUART * q : QUART * (q + 1)])
-
-        def load_wgt(h):
-            nc.sync.dma_start(wgt_sb[:, HALF * h : HALF * (h + 1)], wgt[:, HALF * h : HALF * (h + 1)])
-
-        def load_wt(a):
-            nc.sync.dma_start(wt_raw[a][:], wt[HALF * a : HALF * (a + 1), :].rearrange("(p t) n -> p t n", t=4))
+        def load_c(cols):
+            planes = c.rearrange("(p t) j -> p t j", t=PACK)[:, :, cols[0] : cols[1]]
+            nc.sync.dma_start(buffer("c_raw%d" % cols[0], [P, PACK, cols[1] - cols[0]], F32)[:], planes)
 
         def load_wx():
             nc.sync.dma_start(wx_codes[:].bitcast(I32), wx_words[0].bitcast(I32))
             for quad in range(4):
                 nc.sync.dma_start(
-                    wx_plane[32 * quad : 32 * quad + 4, :].bitcast(I32),
+                    wx_bytes[32 * quad : 32 * quad + 4, :].bitcast(I32),
                     wx_scales[0, 4 * quad : 4 * quad + 4, :].bitcast(I32),
                 )
 
-        load_c(0)
-        load_wgt(0)
-        load_x(0)
-        load_wgt(1)
-        load_x(1)
-        load_c(1)
-        load_x(2)
-        load_c(2)
-        load_x(3)
-        load_c(3)
+        def load_wt(a):
+            planes = wt[PASS * a : PASS * (a + 1), :].rearrange("(p t) n -> p t n", t=PACK)
+            nc.sync.dma_start(buffer("wt_raw%d" % a, [P, PACK, N], F32)[:], planes)
+
+        def load_wgt(cols):
+            nc.sync.dma_start(wgt_sb[:, cols[0] : cols[1]], wgt[:, cols[0] : cols[1]])
+
+        def load_x(plane):
+            a, t = divmod(plane, PACK)
+            planes = xT[PASS * a : PASS * (a + 1), :].rearrange("(p t) w -> p t w", t=PACK)
+            nc.sync.dma_start(buffer("x%d" % plane, [P, T], F32)[:], planes[:, t, :])
+
+        for cols in (FRONT, MIDDLE, LAST):
+            load_c(cols)
         load_wx()
         load_wt(0)
-        load_x(4)
-        load_x(5)
-        load_x(6)
+        load_wgt(FRONT)
+        load_x(0)
+        load_wgt(BACK)
+        load_x(1)
         load_wt(1)
-        load_x(7)
+        for plane in range(2, K // P):
+            load_x(plane)
 
-        def gather(g, a, b):
-            nc.vector.tensor_tensor(
-                picked[g // 4][:, g % 4, a:b],
-                x_planes[g][:].indirect(offsets[:, a // 16 : b // 16]),
-                wgt_sb[:, a:b],
-                MULT,
-            )
+        def c_planes(first, end):
+            base = max(cols[0] for cols in (FRONT, MIDDLE, LAST) if cols[0] <= first)
+            return buffers["c_raw%d" % base][:, :, first - base : end - base]
 
-        def round_c(q):
-            nc.scalar.copy(by_fours(cq[0][:, QUART * q : QUART * (q + 1), :]), planes_by_fours(c_raw[q][:]))
+        def cq_bf(q):
+            return buffer("cq_bf%d" % q, [P, QUARTER, PACK], BF16)
+
+        def cr_bf(h):
+            return buffer("cr_bf%d" % h, [P, HALF, PACK], BF16)
+
+        def weave_c(q, copy):
+            copy(columns_in_runs(cq_bf(q)[:]), planes_in_runs(c_planes(QUARTER * q, QUARTER * (q + 1))))
 
         decoded = {}
 
-        def decode(e):
-            bank = psum.tile([P, HALF], F32, name="dec%d" % e, tag="bank%d" % (4 + e % 4))
-            decoded[e] = bank
-            for t in range(4):
-                nc.tensor.matmul_mx(
-                    out=bank[:, P * t : P * (t + 1)],
-                    lhsT=eye_codes[:, P * t : P * (t + 1)].bitcast(FP8X4),
-                    lhsT_scale=eye_scales[:, P * t : P * (t + 1)],
-                    rhs=cq[1][:, P * e : P * (e + 1)].bitcast(FP8X4),
-                    rhs_scale=cq[2][:, P * e : P * (e + 1)],
-                    start=True,
-                    stop=True,
+        def quantize_cq(q):
+            quantize(cq, (QUARTER * q, QUARTER * (q + 1)), cq_bf(q)[:])
+            for first in range(QUARTER * q, QUARTER * (q + 1), P):
+                decoded[first] = bank_tile("decoded%d" % first, (ROW_TILES + first // P) % BANKS)
+                for t in range(PACK):
+                    result = decoded[first][:, P * t : P * (t + 1)]
+                    matmul(result, e4m3_columns(eye_mx, t), cq, (first, first + P), True, True)
+
+        def subtract_cq(q):
+            for first in range(QUARTER * q, QUARTER * (q + 1), P):
+                nc.vector.tensor_tensor(
+                    columns_in_runs(cr_bf(first // HALF)[:, first % HALF : first % HALF + P, :]),
+                    planes_in_runs(c_planes(first, first + P)),
+                    decoded[first][:].rearrange("p (t c i) -> p c t i", t=PACK, i=RUN),
+                    ALU.subtract,
                 )
 
-        def leftover(e):
-            q, o = divmod(e, 2)
+        def quantize_cr(h):
+            quantize(cr, (HALF * h, HALF * (h + 1)), cr_bf(h)[:])
+
+        def wt_bf(a):
+            return buffer("wt_bf%d" % a, [P, N, PACK], BF16)
+
+        def weave_wt(a):
+            nc.scalar.copy(columns_in_runs(wt_bf(a)[:]), planes_in_runs(buffers["wt_raw%d" % a][:]))
+
+        def quantize_wt(a):
+            quantize(wq[a], (0, N), wt_bf(a)[:])
+
+        def picked(first_plane, end_plane, cols):
+            lo, hi, (base, end) = [e for e in PICKED if e[0] <= first_plane < e[1] and e[2][0] <= cols[0] < e[2][1]][0]
+            tile = buffer("picked%d_%d" % (lo, base), [P, hi - lo, end - base], F32)
+            return tile[:, first_plane - lo : end_plane - lo, cols[0] - base : cols[1] - base]
+
+        def xg_bf(a, cols):
+            base = cols[0] // HALF * HALF
+            return buffer("xg_bf%d_%d" % (a, base), [P, HALF, PACK], BF16)[:, cols[0] - base : cols[1] - base, :]
+
+        def gather(plane, cols):
             nc.vector.tensor_tensor(
-                by_fours(cr[0][:, P * e : P * (e + 1), :]),
-                planes_by_fours(c_raw[q][:, :, P * o : P * (o + 1)]),
-                decoded[e][:].rearrange("p (t c i) -> p c t i", t=4, i=4),
-                SUB,
+                picked(plane, plane + 1, cols)[:, 0, :],
+                buffers["x%d" % plane][:].indirect(offsets[:, cols[0] // LIST_ROWS : cols[1] // LIST_ROWS]),
+                wgt_sb[:, cols[0] : cols[1]],
+                ALU.mult,
             )
 
-        def quant_cq(q):
-            quantize(cq, QUART * q, QUART * (q + 1))
-            decode(2 * q)
-            decode(2 * q + 1)
+        def weave_xg(a, cols, copy):
+            copy(columns_in_runs(xg_bf(a, cols)), planes_in_runs(picked(PACK * a, PACK * (a + 1), cols)))
 
-        def finish_c(q):
-            leftover(2 * q)
-            leftover(2 * q + 1)
+        def weave_xg_pair(plane, cols):
+            a, t = divmod(plane, PACK)
+            nc.scalar.copy(xg_bf(a, cols)[:, :, t : t + 2], picked(plane, plane + 2, cols).rearrange("p t w -> p w t"))
 
-        def round_all(dst, src, a, b):
-            nc.scalar.copy(by_fours(dst[:, a:b, :]), planes_by_fours(src[:, :, a:b]))
+        def quantize_xg(a, cols):
+            quantize(xg[a], cols, xg_bf(a, cols))
 
-        def round_pair(copy, u, a, b):
-            copy(xg[1][0][:, a:b, 2 * u : 2 * u + 2], picked[1][:, 2 * u : 2 * u + 2, a:b].rearrange("p t w -> p w t"))
+        sums = {}
 
-        acc = {}
+        def add_pass(cols, n, stationary, moving, step, stop):
+            for first in range(cols[0], cols[1], step):
+                start = (cols, n) not in sums
+                if start:
+                    sums[cols, n] = bank_tile("sum%d_%d" % (cols[0], n), FIRST_BANK[cols] + n)
+                result = sums[cols, n][:, first - cols[0] : first - cols[0] + step]
+                matmul(result, stationary, moving, (first, first + step), start, stop)
 
-        def wx_pass(h, n, op, start):
-            if start:
-                acc[h, n] = psum.tile([P, HALF], F32, name="acc%d%d" % (h, n), tag="bank%d" % (4 * h + n))
-            nc.tensor.matmul_mx(
-                out=acc[h, n][:],
-                lhsT=wx_codes[:, 2 * P * n : 2 * P * (n + 1)].bitcast(FP4X4),
-                lhsT_scale=wx_plane[:, P * n : P * (n + 1)],
-                rhs=op[1][:, HALF * h : HALF * (h + 1)].bitcast(FP8X4),
-                rhs_scale=op[2][:, HALF * h : HALF * (h + 1)],
-                start=start,
-                stop=False,
-            )
+        def add_wx(tier, cols, row_tiles=range(ROW_TILES)):
+            step = BANK if cols == FRONT else P
+            for n in row_tiles:
+                add_pass(cols, n, wx_columns(n), tier, step, False)
 
-        def wt_pass(a, n, lo, hi, stop):
-            h = lo // HALF
-            nc.tensor.matmul_mx(
-                out=acc[h, n][:, lo - HALF * h : hi - HALF * h],
-                lhsT=wq[a][1][:, P * n : P * (n + 1)].bitcast(FP8X4),
-                lhsT_scale=wq[a][2][:, P * n : P * (n + 1)],
-                rhs=xg[a][1][:, lo:hi].bitcast(FP8X4),
-                rhs_scale=xg[a][2][:, lo:hi],
-                start=False,
-                stop=stop,
-            )
+        def add_wt(a, cols, row_tiles=range(ROW_TILES)):
+            for n in row_tiles:
+                add_pass(cols, n, e4m3_columns(wq[a], n), xg[a], cols[1] - cols[0], a == 1)
 
-        def emit(h, n, copy):
-            copy(staged[4 * h + n][:], acc[h, n][:])
-            nc.sync.dma_start(out[P * n : P * (n + 1), HALF * h : HALF * (h + 1)], staged[4 * h + n][:])
+        def early_wx_sum(n):
+            bank = bank_tile("early%d" % n, FIRST_BANK[MIDDLE] + n)
+            for first in range(LAST[0], LAST[1], P):
+                result = bank[:, first - LAST[0] : first - LAST[0] + P]
+                matmul(result, wx_columns(n), cq, (first, first + P), True, False)
+                matmul(result, wx_columns(n), cr, (first, first + P), False, True)
+            nc.scalar.copy(buffer("early_sum%d" % n, [P, QUARTER], F32)[:], bank[:, 0:QUARTER])
 
-        for q in range(4):
-            round_c(q)
-            quant_cq(q)
-            if q > 0:
-                gather(q - 1, HALF, J)
-            finish_c(q)
-            gather(q, 0, HALF)
-            quantize(cr, QUART * q, QUART * (q + 1))
-        gather(3, HALF, J)
-        for h in range(2):
-            round_all(xg[0][0], picked[0], HALF * h, HALF * (h + 1))
-        round_all(wq[0][0], wt_raw[0], 0, N)
-        for h in range(2):
-            for n in range(4):
-                wx_pass(h, n, cq, True)
-                wx_pass(h, n, cr, False)
-        gather(4, 0, HALF)
-        gather(4, HALF, J)
-        quantize(xg[0], 0, HALF)
-        gather(5, 0, HALF)
-        quantize(xg[0], HALF, J)
-        gather(5, HALF, J)
-        quantize(wq[0], 0, N)
-        for h in range(2):
-            for n in range(4):
-                wt_pass(0, n, HALF * h, HALF * (h + 1), False)
-        round_pair(nc.scalar.copy, 0, 0, J)
-        gather(6, 0, HALF)
-        gather(6, HALF, J)
-        round_all(wq[1][0], wt_raw[1], 0, N)
-        quantize(wq[1], 0, N)
-        for q in range(4):
-            gather(7, QUART * q, QUART * (q + 1))
-        round_pair(nc.scalar.copy, 1, 0, QUART)
-        round_pair(nc.scalar.copy, 1, QUART, HALF)
-        quantize(xg[1], 0, QUART)
-        quantize(xg[1], QUART, HALF)
-        round_pair(nc.vector.tensor_copy, 1, HALF, J)
-        for n in range(4):
-            wt_pass(1, n, 0, QUART, False)
-        for n in range(4):
-            wt_pass(1, n, QUART, HALF, True)
-        quantize(xg[1], HALF, J)
-        for n in range(4):
-            wt_pass(1, n, HALF, J, True)
-        for n in range(4):
-            emit(0, n, nc.scalar.copy)
-        for n in range(4):
-            emit(1, n, nc.vector.tensor_copy if n % 2 == 0 else nc.scalar.copy)
+        def store(cols, n):
+            width = cols[1] - cols[0]
+            staged = buffer("staged%d_%d" % (cols[0], n), [P, width], F32)
+            if cols == LAST and n in ADDED_TILES:
+                nc.vector.tensor_tensor(staged[:], sums[cols, n][:, 0:width], buffers["early_sum%d" % n][:], ALU.add)
+            else:
+                nc.scalar.copy(staged[:], sums[cols, n][:, 0:width])
+            nc.sync.dma_start(out[P * n : P * (n + 1), cols[0] : cols[1]], staged[:])
+
+        weave_c(0, nc.vector.tensor_copy)
+        weave_c(1, nc.scalar.copy)
+        quantize_cq(0)
+        weave_c(2, nc.scalar.copy)
+        quantize_cq(1)
+        weave_c(3, nc.scalar.copy)
+        subtract_cq(0)
+        quantize_cq(2)
+        subtract_cq(1)
+        quantize_cq(3)
+        weave_wt(0)
+        subtract_cq(2)
+
+        gather(0, FRONT)
+        subtract_cq(3)
+        add_wx(cq, FRONT)
+        gather(0, BACK)
+        weave_wt(1)
+        quantize_cr(0)
+        add_wx(cr, FRONT)
+        quantize_wt(0)
+        gather(1, FRONT)
+        gather(1, BACK)
+        quantize_cr(1)
+        for n in ADDED_TILES:
+            early_wx_sum(n)
+        add_wx(cq, MIDDLE)
+        add_wx(cr, MIDDLE)
+        gather(2, FRONT)
+        gather(2, BACK)
+        gather(3, FRONT)
+        quantize_wt(1)
+        weave_xg(0, FRONT, nc.scalar.copy)
+        gather(3, BACK)
+
+        gather(4, FRONT)
+        gather(4, MIDDLE)
+        quantize_xg(0, FRONT)
+        add_wt(0, FRONT)
+        gather(5, FRONT)
+        weave_xg_pair(4, FRONT)
+        gather(5, MIDDLE)
+        weave_xg(0, BACK, nc.scalar.copy)
+        gather(6, FRONT)
+        gather(6, MIDDLE)
+        for cols in ((0, QUARTER), (QUARTER, HALF)):
+            gather(7, cols)
+            weave_xg_pair(6, cols)
+        quantize_xg(0, BACK)
+        add_wt(0, MIDDLE)
+        quantize_xg(1, FRONT)
+        add_wt(1, FRONT)
+        gather(7, MIDDLE)
+        for n in range(ROW_TILES):
+            store(FRONT, n)
+        weave_xg(1, MIDDLE, nc.scalar.copy)
+        for plane in range(PACK, 2 * PACK):
+            gather(plane, LAST)
+        add_wt(0, LAST, PLAIN_TILES)
+        add_wx(cq, LAST, PLAIN_TILES)
+        add_wx(cr, LAST, PLAIN_TILES)
+        quantize_xg(1, MIDDLE)
+        add_wt(1, MIDDLE)
+        weave_xg(1, LAST, nc.vector.tensor_copy)
+        add_wt(0, LAST, ADDED_TILES)
+        quantize_xg(1, LAST)
+        for n in range(ROW_TILES):
+            store(MIDDLE, n)
+        alternating = [n for pair in zip(ADDED_TILES, PLAIN_TILES) for n in pair]
+        add_wt(1, LAST, alternating)
+        for n in alternating:
+            store(LAST, n)

import concourse.mybir as mybir
from concourse.masks import make_identity

K, L, N, T, J = 1024, 512, 512, 2048, 1024
FLOPS = 2 * (K * N * J + 2 * L * N * J + L * L * J)

F32 = mybir.dt.float32
BF16 = mybir.dt.bfloat16
I32 = mybir.dt.int32
U32 = mybir.dt.uint32
U16 = mybir.dt.uint16
U8 = mybir.dt.uint8
FP8X4 = mybir.dt.float8_e4m3fn_x4
FP4X4 = mybir.dt.float4_e2m1fn_x4
ALU = mybir.AluOpType

P = 128
PACK = 4
PASS = P * PACK
BANK = 512
BANKS = 8
ROW_TILES = N // P
LIST_ROWS = 16
RUN = 4
HALF = J // 2
QUARTER = J // 4

FRONT, MIDDLE, LAST = (0, HALF), (HALF, HALF + QUARTER), (HALF + QUARTER, J)
BACK = (HALF, J)
FIRST_BANK = {FRONT: 0, MIDDLE: ROW_TILES, LAST: 0}
ADDED_TILES, PLAIN_TILES = (2, 3), (0, 1)

PICKED = [(0, 4, FRONT), (0, 4, BACK), (4, 6, FRONT), (6, 8, FRONT), (4, 8, MIDDLE), (4, 8, LAST)]

TAKES_BYTES_OF = {
    "cq_bf0": "eye_bf",
    "cq_bf1": "eye",
    "cq_bf2": "cq_bf0",
    "cq_bf3": "cq_bf1",
    "wt_bf0": "cq_bf3",
    "wt_bf1": "x0",
    "picked0_0": "c_raw512",
    "picked0_512": "c_raw768",
    "picked4_0": "x1",
    "picked4_512": "x2",
    "picked6_0": "xg_bf0_0",
    "picked4_768": "picked6_0",
}


def tile_list_none_kernel(tc, xT, wgt, wt, c, wx_words, wx_scales, offs, out):
    nc = tc.nc
    with tc.tile_pool(name="keep", bufs=1) as keep, tc.psum_pool(name="psum", bufs=1) as psum:
        offsets = keep.tile([P, J // LIST_ROWS], U16, name="offsets")
        nc.sync.dma_start(offsets[:], offs)

        buffers = {}

        def buffer(name, shape, dtype):
            if name not in buffers:
                tag = name
                while tag in TAKES_BYTES_OF:
                    tag = TAKES_BYTES_OF[tag]
                buffers[name] = keep.tile(shape, dtype, name=name, tag=tag, align_bytes=64)
            return buffers[name]

        def bank_tile(name, bank):
            return psum.tile([P, BANK], F32, name=name, tag="bank%d" % bank)

        def mx_operand(name, width):
            codes = keep.tile([P, width], U32, name=name + "_codes", align_bytes=64)
            scales = keep.tile([P, width], U8, name=name + "_scales", align_bytes=64)
            return codes, scales

        def quantize(operand, cols, woven):
            codes, scales = operand
            nc.vector.quantize_mx(
                out=codes[:, cols[0] : cols[1]].bitcast(FP8X4),
                scales=scales[:, cols[0] : cols[1]],
                in_=woven.rearrange("p w t -> p (w t)"),
            )

        def columns_in_runs(woven):
            return woven.rearrange("p (c i) t -> p c t i", i=RUN)

        def planes_in_runs(planes):
            return planes.rearrange("p t (c i) -> p c t i", i=RUN)

        def matmul(result, stationary, moving, cols, start, stop):
            nc.tensor.matmul_mx(
                out=result,
                lhsT=stationary[0],
                lhsT_scale=stationary[1],
                rhs=moving[0][:, cols[0] : cols[1]].bitcast(FP8X4),
                rhs_scale=moving[1][:, cols[0] : cols[1]],
                start=start,
                stop=stop,
            )

        def e4m3_columns(operand, n):
            return operand[0][:, P * n : P * (n + 1)].bitcast(FP8X4), operand[1][:, P * n : P * (n + 1)]

        wgt_sb = keep.tile([P, J], F32, name="wgt_sb")
        wx_codes = keep.tile([P, 2 * N], U8, name="wx_codes", align_bytes=256)
        wx_bytes = keep.tile([P, N], U8, name="wx_bytes", align_bytes=64)
        xg = [mx_operand("xg%d" % a, J) for a in range(K // PASS)]
        wq = [mx_operand("wq%d" % a, N) for a in range(K // PASS)]
        cq = mx_operand("cq", J)
        cr = mx_operand("cr", J)

        def wx_columns(n):
            return wx_codes[:, 2 * P * n : 2 * P * (n + 1)].bitcast(FP4X4), wx_bytes[:, P * n : P * (n + 1)]

        eye = buffer("eye", [P, P], BF16)
        eye_bf = buffer("eye_bf", [P, PACK * PASS], BF16)
        eye_mx = mx_operand("eye", PASS)
        nc.gpsimd.memset(eye_bf[:, 0:PASS].bitcast(I32), 0)
        make_identity(nc, eye[:])
        nc.vector.memset(eye_bf[:, PASS:].bitcast(I32), 0)
        nc.vector.memset(wx_bytes[:].bitcast(I32), 0)
        for t in range(PACK):
            copy = nc.scalar.copy if t == 0 else nc.vector.tensor_copy
            copy(eye_bf[:, PASS * t + t : PASS * (t + 1) : PACK], eye[:])
        nc.vector.quantize_mx(out=eye_mx[0][:].bitcast(FP8X4), scales=eye_mx[1][:], in_=eye_bf[:])

        def load_c(cols):
            planes = c.rearrange("(p t) j -> p t j", t=PACK)[:, :, cols[0] : cols[1]]
            nc.sync.dma_start(buffer("c_raw%d" % cols[0], [P, PACK, cols[1] - cols[0]], F32)[:], planes)

        def load_wx():
            nc.sync.dma_start(wx_codes[:].bitcast(I32), wx_words[0].bitcast(I32))
            for quad in range(4):
                nc.sync.dma_start(
                    wx_bytes[32 * quad : 32 * quad + 4, :].bitcast(I32),
                    wx_scales[0, 4 * quad : 4 * quad + 4, :].bitcast(I32),
                )

        def load_wt(a):
            planes = wt[PASS * a : PASS * (a + 1), :].rearrange("(p t) n -> p t n", t=PACK)
            nc.sync.dma_start(buffer("wt_raw%d" % a, [P, PACK, N], F32)[:], planes)

        def load_wgt(cols):
            nc.sync.dma_start(wgt_sb[:, cols[0] : cols[1]], wgt[:, cols[0] : cols[1]])

        def load_x(plane):
            a, t = divmod(plane, PACK)
            planes = xT[PASS * a : PASS * (a + 1), :].rearrange("(p t) w -> p t w", t=PACK)
            nc.sync.dma_start(buffer("x%d" % plane, [P, T], F32)[:], planes[:, t, :])

        for cols in (FRONT, MIDDLE, LAST):
            load_c(cols)
        load_wx()
        load_wt(0)
        load_wgt(FRONT)
        load_x(0)
        load_wgt(BACK)
        load_x(1)
        load_wt(1)
        for plane in range(2, K // P):
            load_x(plane)

        def c_planes(first, end):
            base = max(cols[0] for cols in (FRONT, MIDDLE, LAST) if cols[0] <= first)
            return buffers["c_raw%d" % base][:, :, first - base : end - base]

        def cq_bf(q):
            return buffer("cq_bf%d" % q, [P, QUARTER, PACK], BF16)

        def cr_bf(h):
            return buffer("cr_bf%d" % h, [P, HALF, PACK], BF16)

        def weave_c(q, copy):
            copy(columns_in_runs(cq_bf(q)[:]), planes_in_runs(c_planes(QUARTER * q, QUARTER * (q + 1))))

        decoded = {}

        def quantize_cq(q):
            quantize(cq, (QUARTER * q, QUARTER * (q + 1)), cq_bf(q)[:])
            for first in range(QUARTER * q, QUARTER * (q + 1), P):
                decoded[first] = bank_tile("decoded%d" % first, (ROW_TILES + first // P) % BANKS)
                for t in range(PACK):
                    result = decoded[first][:, P * t : P * (t + 1)]
                    matmul(result, e4m3_columns(eye_mx, t), cq, (first, first + P), True, True)

        def subtract_cq(q):
            for first in range(QUARTER * q, QUARTER * (q + 1), P):
                nc.vector.tensor_tensor(
                    columns_in_runs(cr_bf(first // HALF)[:, first % HALF : first % HALF + P, :]),
                    planes_in_runs(c_planes(first, first + P)),
                    decoded[first][:].rearrange("p (t c i) -> p c t i", t=PACK, i=RUN),
                    ALU.subtract,
                )

        def quantize_cr(h):
            quantize(cr, (HALF * h, HALF * (h + 1)), cr_bf(h)[:])

        def wt_bf(a):
            return buffer("wt_bf%d" % a, [P, N, PACK], BF16)

        def weave_wt(a):
            nc.scalar.copy(columns_in_runs(wt_bf(a)[:]), planes_in_runs(buffers["wt_raw%d" % a][:]))

        def quantize_wt(a):
            quantize(wq[a], (0, N), wt_bf(a)[:])

        def picked(first_plane, end_plane, cols):
            lo, hi, (base, end) = [e for e in PICKED if e[0] <= first_plane < e[1] and e[2][0] <= cols[0] < e[2][1]][0]
            tile = buffer("picked%d_%d" % (lo, base), [P, hi - lo, end - base], F32)
            return tile[:, first_plane - lo : end_plane - lo, cols[0] - base : cols[1] - base]

        def xg_bf(a, cols):
            base = cols[0] // HALF * HALF
            return buffer("xg_bf%d_%d" % (a, base), [P, HALF, PACK], BF16)[:, cols[0] - base : cols[1] - base, :]

        def gather(plane, cols):
            nc.vector.tensor_tensor(
                picked(plane, plane + 1, cols)[:, 0, :],
                buffers["x%d" % plane][:].indirect(offsets[:, cols[0] // LIST_ROWS : cols[1] // LIST_ROWS]),
                wgt_sb[:, cols[0] : cols[1]],
                ALU.mult,
            )

        def weave_xg(a, cols, copy):
            copy(columns_in_runs(xg_bf(a, cols)), planes_in_runs(picked(PACK * a, PACK * (a + 1), cols)))

        def weave_xg_pair(plane, cols):
            a, t = divmod(plane, PACK)
            nc.scalar.copy(xg_bf(a, cols)[:, :, t : t + 2], picked(plane, plane + 2, cols).rearrange("p t w -> p w t"))

        def quantize_xg(a, cols):
            quantize(xg[a], cols, xg_bf(a, cols))

        sums = {}

        def add_pass(cols, n, stationary, moving, step, stop):
            for first in range(cols[0], cols[1], step):
                start = (cols, n) not in sums
                if start:
                    sums[cols, n] = bank_tile("sum%d_%d" % (cols[0], n), FIRST_BANK[cols] + n)
                result = sums[cols, n][:, first - cols[0] : first - cols[0] + step]
                matmul(result, stationary, moving, (first, first + step), start, stop)

        def add_wx(tier, cols, row_tiles=range(ROW_TILES)):
            step = BANK if cols == FRONT else P
            for n in row_tiles:
                add_pass(cols, n, wx_columns(n), tier, step, False)

        def add_wt(a, cols, row_tiles=range(ROW_TILES)):
            for n in row_tiles:
                add_pass(cols, n, e4m3_columns(wq[a], n), xg[a], cols[1] - cols[0], a == 1)

        def early_wx_sum(n):
            bank = bank_tile("early%d" % n, FIRST_BANK[MIDDLE] + n)
            for first in range(LAST[0], LAST[1], P):
                result = bank[:, first - LAST[0] : first - LAST[0] + P]
                matmul(result, wx_columns(n), cq, (first, first + P), True, False)
                matmul(result, wx_columns(n), cr, (first, first + P), False, True)
            nc.scalar.copy(buffer("early_sum%d" % n, [P, QUARTER], F32)[:], bank[:, 0:QUARTER])

        def store(cols, n):
            width = cols[1] - cols[0]
            staged = buffer("staged%d_%d" % (cols[0], n), [P, width], F32)
            if cols == LAST and n in ADDED_TILES:
                nc.vector.tensor_tensor(staged[:], sums[cols, n][:, 0:width], buffers["early_sum%d" % n][:], ALU.add)
            else:
                nc.scalar.copy(staged[:], sums[cols, n][:, 0:width])
            nc.sync.dma_start(out[P * n : P * (n + 1), cols[0] : cols[1]], staged[:])

        weave_c(0, nc.vector.tensor_copy)
        weave_c(1, nc.scalar.copy)
        quantize_cq(0)
        weave_c(2, nc.scalar.copy)
        quantize_cq(1)
        weave_c(3, nc.scalar.copy)
        subtract_cq(0)
        quantize_cq(2)
        subtract_cq(1)
        quantize_cq(3)
        weave_wt(0)
        subtract_cq(2)

        gather(0, FRONT)
        subtract_cq(3)
        add_wx(cq, FRONT)
        gather(0, BACK)
        weave_wt(1)
        quantize_cr(0)
        add_wx(cr, FRONT)
        quantize_wt(0)
        gather(1, FRONT)
        gather(1, BACK)
        quantize_cr(1)
        for n in ADDED_TILES:
            early_wx_sum(n)
        add_wx(cq, MIDDLE)
        add_wx(cr, MIDDLE)
        gather(2, FRONT)
        gather(2, BACK)
        gather(3, FRONT)
        quantize_wt(1)
        weave_xg(0, FRONT, nc.scalar.copy)
        gather(3, BACK)

        gather(4, FRONT)
        gather(4, MIDDLE)
        quantize_xg(0, FRONT)
        add_wt(0, FRONT)
        gather(5, FRONT)
        weave_xg_pair(4, FRONT)
        gather(5, MIDDLE)
        weave_xg(0, BACK, nc.scalar.copy)
        gather(6, FRONT)
        gather(6, MIDDLE)
        for cols in ((0, QUARTER), (QUARTER, HALF)):
            gather(7, cols)
            weave_xg_pair(6, cols)
        quantize_xg(0, BACK)
        add_wt(0, MIDDLE)
        quantize_xg(1, FRONT)
        add_wt(1, FRONT)
        gather(7, MIDDLE)
        for n in range(ROW_TILES):
            store(FRONT, n)
        weave_xg(1, MIDDLE, nc.scalar.copy)
        for plane in range(PACK, 2 * PACK):
            gather(plane, LAST)
        add_wt(0, LAST, PLAIN_TILES)
        add_wx(cq, LAST, PLAIN_TILES)
        add_wx(cr, LAST, PLAIN_TILES)
        quantize_xg(1, MIDDLE)
        add_wt(1, MIDDLE)
        weave_xg(1, LAST, nc.vector.tensor_copy)
        add_wt(0, LAST, ADDED_TILES)
        quantize_xg(1, LAST)
        for n in range(ROW_TILES):
            store(MIDDLE, n)
        alternating = [n for pair in zip(ADDED_TILES, PLAIN_TILES) for n in pair]
        add_wt(1, LAST, alternating)
        for n in alternating:
            store(LAST, n)
